import numpy as np, ml_dtypes
CORES = [35,38,43,46]
N = 4
import mx_ref
BF = ml_dtypes.bfloat16
def entries(a):
    return np.ascontiguousarray(a.T).reshape(-1)
def table(e):
    return np.ascontiguousarray(np.reshape(e, (-1, 16)).T).astype(np.int32)
def cols(t, e):
    v = np.concatenate([t.reshape(128, -1, 4), np.zeros((128, 1, 4), BF)], axis=1)
    return np.ascontiguousarray(v[:, e]).reshape(128, -1)
def cut(t, i, w=512):
    return t[:, w * i:w * i + w]
def f(rng, *shape):
    return mx_ref.flush((rng.standard_normal(shape, dtype=np.float32) * np.exp2(rng.integers(-2, 3, shape[:-1] + (1,)))).astype(BF))
def wide(rng, *shape, cols=0):
    v = rng.standard_normal(shape, dtype=np.float32) * np.exp2(rng.integers(-12, 13, shape)).astype(np.float32)
    if cols: v *= np.repeat(np.exp2(rng.integers(-cols, cols + 1, shape[:-2] + (1, shape[-1] // 4))) * (rng.random(shape[:-2] + (1, shape[-1] // 4)) > 0.0625), 4, axis=-1).astype(np.float32)
    return mx_ref.flush(v.astype(BF))
TB, T, CAPP, O = 512, 512, 64, 2
def lists(rng, case=""):
    o = []; odd = rng.permutation(N)
    for r in range(N):
        lo, hi = {"one": (1, 1), "full": (CAPP, CAPP), "runs": (1, CAPP // 2), "none": (1, CAPP)}.get(case, (0, CAPP))
        n = rng.integers(lo, hi + 1, N)
        if case == "none":
            if r == odd[0]: n[:] = 0; n[rng.integers(0, N)] = 1
            elif r == odd[1]: n[r] = 0
            elif r == odd[2]: n[np.arange(N) != r] = 0
            else: n[rng.permutation(N)[:rng.integers(1, N)]] = 0
        if n.sum() == 0: n[rng.integers(0, N)] = 1
        if case == "full": named = [np.append([0, TB - 1], 1 + rng.permutation(TB - 2)[:n[q] - 2]) for q in range(N)]
        else: named = [rng.permutation(TB)[:n[q]] for q in range(N)]
        pool = rng.permutation(np.concatenate([q * TB + named[q] for q in range(N)]))
        i = np.arange(len(pool))
        k = T - len(pool)
        i = np.concatenate([i, (rng.random(k) * rng.random(k) * len(pool)).astype(int)])
        i = np.sort(i) if case == "runs" else rng.permutation(i)
        o.append(table(pool[i]))
    return {"want": np.stack(o)}
def setup_inputs(rng):
    return {"x": f(rng, N, 128, 4 * TB), "w": f(rng, N, 128, 512 * O), **lists(rng)}
def setup_inputs_one(rng):
    return {**setup_inputs(rng), **lists(rng, "one")}
def setup_inputs_full(rng):
    return {**setup_inputs(rng), **lists(rng, "full")}
def setup_inputs_runs(rng):
    return {**setup_inputs(rng), **lists(rng, "runs")}
def setup_inputs_none(rng):
    return {**setup_inputs(rng), **lists(rng, "none")}
def setup_inputs_spread(rng):
    d = setup_inputs(rng); d["x"] = wide(rng, N, 128, 4 * TB, cols=8); return d
def check_inputs(d):
    b = []
    for r in range(N):
        e = entries(d["want"][r])
        if e.min() < 0 or e.max() >= N * TB or any(len(np.unique(e[e // TB == q])) > CAPP for q in range(N)): b.append("want")
    return b
def reference(x, w, want):
    every = np.concatenate([x[q] for q in range(N)], axis=1)
    y = np.zeros((N, 128, O * T), np.float32)
    for r in range(N):
        t = mx_ref.quantize(cols(every, entries(want[r])))
        for o in range(O):
            y[r][:, T * o:T * o + T] = mx_ref.matmul(mx_ref.quantize(np.ascontiguousarray(cut(w[r], o))), t)
    return {"y": y}

@@ -1,0 +1,338 @@
+from concourse.bass import DstId, RemoteDMATransfer
+from concourse.mybir import dt, AluOpType, AxisListType, ActivationFunctionType
+
+A = AluOpType
+F = ActivationFunctionType
+ROW = "float16"
+HS = 192
+
+SCRATCH = {
+    "wl": ("sbuf", [128, 4], "int32"),
+    "wl16": ("sbuf", [128, 32], "int32"),
+    "pi": ("sbuf", [128, 1], "int32"),
+    "ci": ("sbuf", [128, 4], "float32"),
+    "mi": ("sbuf", [128, 4], "float32"),
+    "i31": ("sbuf", [128, 1], "int32"),
+    "i15": ("sbuf", [128, 1], "int32"),
+    "i31f": ("sbuf", [128, 1], "float32"),
+    "i15f": ("sbuf", [128, 1], "float32"),
+    "mp": ("sbuf", [128, 4], "float32"),
+    "kc": ("sbuf", [128, 4], "float32"),
+    "kk": ("sbuf", [128, 4], "float32"),
+    "s4": ("sbuf", [128, 4], "float32"),
+    "sb4": ("sbuf", [128, 4], "float32"),
+    "qcol": ("sbuf", [128, 1], "float32"),
+    "base": ("sbuf", [128, 1], "float32"),
+    "zeros": ("sbuf", [128, 528], "bfloat16"),
+    "big": ("sbuf", [128, 512], "bfloat16"),
+    "ones": ("sbuf", [128, 64], "bfloat16"),
+    "wf": ("sbuf", [128, 4], "float32"),
+    "b1": ("sbuf", [128, 128], ROW),
+    "row": ("sbuf", [128, 128], ROW),
+    "ne": ("sbuf", [128, 512], "bfloat16"),
+    "dist": ("sbuf", [128, 512], "bfloat16"),
+    "soff": ("sbuf", [128, 4], "uint16"),
+    "win": ("sbuf", [128, 2112], "bfloat16"),
+    "wint": ("sbuf", [128, 2048], "bfloat16"),
+    "eo": ("sbuf", [128, 64], "float32"),
+    "e01": ("sbuf", [128, 64], "float32"),
+    "e23": ("sbuf", [128, 64], "float32"),
+    "cn": ("sbuf", [128, 16], "float32"),
+    "b2": ("sbuf", [128, 512], "bfloat16"),
+    "row2": ("sbuf", [128, 512], "bfloat16"),
+    "pp": ("sbuf", [128, 512], "bfloat16"),
+    "junk": ("sbuf", [128, 1536], "bfloat16"),
+    "mk3": ("sbuf", [128, 512], "bfloat16"),
+    "mk2": ("sbuf", [128, 336], "bfloat16"),
+    "zz": ("sbuf", [128, 4], "float32"),
+    "xx": ("sbuf", [128, 4], "float32"),
+    "req": ("sbuf", [128, 4], "float32"),
+    "reqs": ("sbuf", [128, 12], "float32"),
+    "lown": ("sbuf", [128, 4], "uint16"),
+    "lrecv": ("sbuf", [128, 12], "uint16"),
+    "nn": ("sbuf", [128, 32], "int32"),
+    "qd": ("sbuf", [128, 32], "int32"),
+    "n5": ("sbuf", [128, 32], "float32"),
+    "ee": ("sbuf", [128, 32], "float32"),
+    "pm": ("sbuf", [128, 32], "float32"),
+    "off": ("sbuf", [128, 64], "uint16"),
+    "pb": ("sbuf", [128, 528], "bfloat16"),
+    "gs": ("sbuf", [128, 1024], "bfloat16"),
+    "tg": ("sbuf", [128, 1024], "bfloat16"),
+    "sa": ("sbuf", [128, 32], "float32"),
+    "sb": ("sbuf", [128, 32], "float32"),
+    "sc": ("sbuf", [128, 32], "float32"),
+    "slot": ("sbuf", [128, 32], "uint16"),
+    "xs": ("sbuf", [128, 2048], "bfloat16"),
+    "xp": ("sbuf", [128, 2048], "bfloat16"),
+    "tile": ("sbuf", [128, 1024], "bfloat16"),
+    "wt": ("sbuf", [128, 1024], "bfloat16"),
+    "wq": ("sbuf", [128, 256], "float8_e4m3fn_x4"),
+    "wsc": ("sbuf", [128, 256], "uint8"),
+    "qx": ("sbuf", [128, 448], "float8_e4m3fn_x4"),
+    "qs": ("sbuf", [128, 448], "uint8"),
+    "prod": ("psum", [128, 2048], "float32"),
+    "res": ("sbuf", [128, 512], "float32"),
+    "yt": ("sbuf", [128, 1024], "float32"),
+}
+SEMAPHORES = ["v", "s", "pe", "gi", "wl", "wl16", "x", "w", "y", "lists", "local", "arr_a", "arr_b"]
+
+
+def rank_program(g, core, T, topo):
+    me = T.rank_of(core)
+    if me is None:
+        return
+    cores = T.cores
+    S = T.sem
+
+    def near(q):
+        return topo.chip(cores[q]) == topo.chip(core)
+
+    def order(r):
+        o = [q for q in range(len(cores)) if q != r]
+        return sorted(o, key=lambda q: (topo.chip(cores[q]) != topo.chip(cores[r]), (q - r) % len(cores)))
+
+    mine = order(me)
+    away = [q for q in mine if not near(q)]
+    share = {}
+    far = []
+    for k, q in enumerate(away):
+        far = topo.engines(core, cores[q])
+        w = len(far) // len(away)
+        share[q] = far[k * w:(k + 1) * w]
+    for q in mine:
+        if q not in share:
+            share[q] = [e for e in topo.engines(core, cores[q]) if e not in far]
+    masks = {q: sum(1 << e for e in share[q]) for q in mine}
+    n_near = sum(len(share[q]) for q in mine if near(q))
+    n_away = sum(len(share[q]) for q in away)
+
+    def dst(q):
+        rid, pid, _ = topo.addr(cores[q])
+        return [DstId(rid=rid, pnc=pid)]
+
+    cnt = {"v": 0, "s": 0}
+
+    def v(ins):
+        cnt["v"] += 1
+        ins.then_inc(S.v, 1)
+        return cnt["v"]
+
+    def s(ins):
+        cnt["s"] += 1
+        ins.then_inc(S.s, 1)
+        return cnt["s"]
+
+    V, SC, X = g.vector, g.scalar, AxisListType.X
+
+    g.sync.dma_start(T.wl[:], T.want[:]).then_inc(S.wl, 16)
+    g.sync.dma_start(T.xs[:], T.x[:]).then_inc(S.x, 16)
+    g.sync.dma_start(T.wt[:], T.w[:]).then_inc(S.w, 16)
+    for a in range(8):
+        g.sync.dma_start(T.wl16[16 * a:16 * a + 16, :], T.want[:]).then_inc(S.wl16, 16)
+
+    g.iota(T.pi[:], [[1, 1]], 0, 1).then_inc(S.gi, 1)
+    g.iota(T.ci[:], [[16, 4]], 0, 0, allow_small_or_imprecise_dtypes=True).then_inc(S.gi, 1)
+    g.iota(T.mi[:], [[-32, 4]], 128, 0, allow_small_or_imprecise_dtypes=True).then_inc(S.gi, 1)
+    i_z = v(V.memset(T.zeros[:], 0.0))
+    V.wait_ge(S.gi, 3)
+    v(V.tensor_scalar(T.i31[:], T.pi[:], 31, None, A.bitwise_and))
+    i = v(V.tensor_scalar(T.i15[:], T.pi[:], 15, None, A.bitwise_and))
+    v(V.memset(T.big[:], 4096.0))
+    V.wait_ge(S.v, i)
+    v(V.tensor_copy(T.i31f[:], T.i31[:]))
+    i = v(V.tensor_copy(T.i15f[:], T.i15[:]))
+    v(V.memset(T.ones[:], 1.0))
+    V.wait_ge(S.v, i)
+    i = v(V.tensor_scalar(T.mp[:], T.mi[:], T.i31f[:, 0:1], None, A.subtract))
+    v(V.tensor_scalar(T.s4[:], T.ci[:], T.i15f[:, 0:1], None, A.add))
+    v(V.tensor_scalar(T.sb4[:], T.ci[:], T.i15f[:, 0:1], 0.5, A.add, A.add))
+    V.wait_ge(S.v, i)
+    i_const = v(V.tensor_scalar(T.kc[:], T.mp[:], -4096.0, 64.0, A.mult, A.add))
+    i_win = v(V.memset(T.win[:, 0:1056], 0.0))
+    SC.wait_ge(S.v, i_z)
+    for k in range(2):
+        j_win = s(SC.activation(T.win[:, 1056 + 528 * k:1584 + 528 * k], T.zeros[:], F.Copy))
+
+    V.wait_ge(S.wl, 16)
+    i = v(V.tensor_copy(T.wf[:], T.wl[:]))
+    V.wait_ge(S.v, i)
+    for c in range(4):
+        i = v(V.tensor_scalar(T.b1[:, 32 * c:32 * c + 32], T.zeros[:, 0:32], T.wf[:, c:c + 1], None, A.add))
+    V.wait_ge(S.v, i)
+    i = v(V.transpose(T.row[:], T.b1[:]))
+    v(V.tensor_tensor(T.kk[:], T.wf[:], T.kc[:], A.add))
+    V.wait_ge(S.v, i)
+    for c in range(4):
+        i = v(V.tensor_scalar(T.ne[:, 128 * c:128 * c + 128], T.row[:], T.wf[:, c:c + 1], None, A.not_equal))
+    V.wait_ge(S.v, i)
+    i = v(V.tensor_tensor_scan(T.dist[:], T.ne[:], T.big[:], 0.0, A.mult, A.add))
+    V.wait_ge(S.v, i)
+    for c in range(4):
+        i = v(V.tensor_scalar(T.soff[:, c:c + 1], T.dist[:, 128 * c + 127:128 * c + 128], T.kk[:, c:c + 1], T.s4[:, c:c + 1], A.add, A.max))
+    V.wait_ge(S.v, i)
+    V.wait_ge(S.s, j_win)
+    i = v(V.tensor_copy(T.win[:, 0:2112].indirect(T.soff[:, 0:4]), T.ones[:]))
+
+    V.wait_ge(S.v, i)
+    i = v(V.transpose(T.wint[:], T.win[:, 64:2112]))
+    V.wait_ge(S.v, i)
+    i = v(V.tensor_tensor(T.eo[:], T.wint[:, 0:2048:32], T.wint[:, 16:2048:32], A.add))
+    V.wait_ge(S.v, i)
+    v(V.tensor_tensor(T.e01[0:32, :], T.eo[0:32, :], T.eo[32:64, :], A.add))
+    i = v(V.tensor_tensor(T.e23[0:32, :], T.eo[64:96, :], T.eo[96:128, :], A.add))
+    V.wait_ge(S.v, i)
+    for q in range(4):
+        c = slice(16 * q, 16 * q + 16)
+        i_cn = v(V.tensor_tensor(T.cn[32 * q:32 * q + 32, :], T.e01[0:32, c], T.e23[0:32, c], A.add))
+    SC.wait_ge(S.v, i_cn)
+    for b in range(8, 16):
+        j = s(SC.activation(T.b2[:, 32 * b:32 * b + 32], T.zeros[:, 0:32], F.Sign, bias=T.cn[:, b:b + 1]))
+    V.wait_ge(S.v, i_cn)
+    for b in range(8):
+        i = v(V.tensor_scalar(T.b2[:, 32 * b:32 * b + 32], T.zeros[:, 0:32], T.cn[:, b:b + 1], 1.0, A.add, A.min))
+    V.wait_ge(S.v, i)
+    V.wait_ge(S.s, j)
+    i = v(V.transpose(T.row2[:], T.b2[:]))
+    v(V.memset(T.mk2[:, 512 - HS:513 - HS], float(HS)))
+    v(V.memset(T.xx[:, 0:2], 512.0))
+    v(V.memset(T.zz[:, 3:4], 0.0))
+    V.wait_ge(S.v, i)
+    i_p = v(V.tensor_tensor_scan(T.pp[:], T.row2[:], T.zeros[:, 0:512], 0.0, A.add, A.add))
+
+    SC.wait_ge(S.v, i_p)
+    for c in range(3):
+        n = 512 if c < 2 else HS
+        j_cnt = s(SC.activation(T.junk[:, 512 * c:512 * c + n], T.pp[:, 0:n], F.Sign, bias=T.sb4[:, c:c + 1], scale=-1.0, accum_out=T.zz[:, c:c + 1]))
+    V.wait_ge(S.v, i_p)
+    i3 = v(V.tensor_scalar(T.mk3[:], T.pp[:], T.s4[:, 3:4], 2.0, A.is_le, A.mult))
+    i2 = v(V.tensor_scalar(T.mk2[:, 0:512 - HS], T.pp[:, HS:512], T.s4[:, 2:3], 2.0, A.is_le, A.mult))
+    V.wait_ge(S.v, i3)
+    v(V.tensor_reduce(T.xx[:, 3:4], T.mk3[:], X, A.add))
+    V.wait_ge(S.v, i2)
+    i = v(V.tensor_reduce(T.xx[:, 2:3], T.mk2[:, 0:513 - HS], X, A.add))
+    V.wait_ge(S.v, i)
+    V.wait_ge(S.s, j_cnt)
+    i_req = v(V.tensor_tensor(T.req[:], T.zz[:], T.xx[:], A.add))
+
+    g.wait_ge(S.v, i_req)
+    tr = []
+    for q in mine:
+        at = 4 * order(q).index(me)
+        tr.append(RemoteDMATransfer(dst_ids=dst(q), dma_engine_mask=masks[q], remote_sem=S.lists,
+                                    src=T.req[:], dst=T.reqs[:, at:at + 4]))
+    g.remote_dma_fused(tr, local_sem=S.local)
+
+    V.wait_ge(S.x, 16)
+    SC.wait_ge(S.x, 16)
+    for t in range(2):
+        i_xp = v(V.tensor_copy(T.xp[:, 512 * t:512 * t + 512], T.xs[:, t:2048:4]))
+    for t in range(2, 4):
+        j_xp = s(SC.activation(T.xp[:, 512 * t:512 * t + 512], T.xs[:, t:2048:4], F.Copy))
+    V.wait_ge(S.v, i_req)
+    for a in range(4):
+        i_own = v(V.tensor_scalar(T.lown[32 * a:32 * a + 32, :], T.req[32 * me:32 * me + 32, :], 0.5, 511.0, A.mult, A.min))
+    V.wait_ge(S.v, i_own)
+    for t in range(2):
+        v(V.tensor_copy(T.tile[:, 768 + t:1024:4], T.xp[:, 512 * t:512 * t + 512].indirect(T.lown[:, 0:4])))
+    SC.wait_ge(S.s, j_xp)
+    SC.wait_ge(S.v, i_own)
+    for t in range(2, 4):
+        s(SC.activation(T.tile[:, 768 + t:1024:4], T.xp[:, 512 * t:512 * t + 512].indirect(T.lown[:, 0:4]), F.Copy))
+    V.wait_ge(S.w, 16)
+    i_wq = v(V.quantize_mx(T.wq[:, 0:256], T.wsc[:, 0:256], T.wt[:]))
+    for q in range(4):
+        p = slice(32 * q, 32 * q + 32)
+        v(V.memset(T.qcol[p, :], float(q)))
+        k = 0 if q == me else 1 + mine.index(q)
+        i_base = v(V.memset(T.base[p, :], 64.0 * k - 1.0))
+    v(V.memset(T.pb[:, 512:528], 0.0))
+    V.wait_ge(S.wl16, 128)
+    v(V.tensor_scalar(T.nn[:], T.wl16[:], 511, None, A.bitwise_and))
+    i = v(V.tensor_scalar(T.qd[:], T.wl16[:], 9, None, A.logical_shift_right))
+    V.wait_ge(S.v, i)
+    v(V.tensor_scalar(T.n5[:], T.nn[:], -512.0, None, A.add))
+    i = v(V.tensor_scalar(T.ee[:], T.qd[:], T.qcol[:, 0:1], None, A.is_equal))
+    V.wait_ge(S.v, i)
+    i = v(V.tensor_tensor(T.pm[:], T.n5[:], T.ee[:], A.mult))
+    V.wait_ge(S.v, i)
+    v(V.tensor_scalar(T.off[:, 0:64:2], T.pm[:], 512.0, None, A.add))
+    i_off = v(V.tensor_scalar(T.off[:, 1:64:2], T.pm[:], 512.0, None, A.add))
+    SC.wait_ge(S.v, i_base)
+    j_pb = s(SC.activation(T.pb[:, 0:512], T.pp[:], F.Identity, bias=T.base[:, 0:1]))
+
+    V.wait_ge(S.lists, n_near + n_away)
+    for a in range(4):
+        i_l = v(V.tensor_scalar(T.lrecv[32 * a:32 * a + 32, :], T.reqs[32 * me:32 * me + 32, :], 0.5, 511.0, A.mult, A.min))
+    SC.wait_ge(S.v, i_l)
+    V.wait_ge(S.v, i_l)
+    for t in range(2):
+        i = v(V.tensor_copy(T.tile[:, t:768:4], T.xp[:, 512 * t:512 * t + 512].indirect(T.lrecv[:, 0:12])))
+    for t in range(2, 4):
+        j = s(SC.activation(T.tile[:, t:768:4], T.xp[:, 512 * t:512 * t + 512].indirect(T.lrecv[:, 0:12]), F.Copy))
+    V.wait_ge(S.v, i)
+    V.wait_ge(S.s, j)
+    i_q = v(V.quantize_mx(T.qx[:, 0:256], T.qs[:, 0:256], T.tile[:]))
+
+    g.wait_ge(S.v, i_q)
+    for codes in (True, False):
+        tr = []
+        for k, q in enumerate(mine):
+            at = 256 + 64 * order(q).index(me)
+            if codes:
+                a, b = T.qx[:, 64 * k:64 * k + 64].bitcast(dt.uint8), T.qx[:, at:at + 64].bitcast(dt.uint8)
+            else:
+                a, b = T.qs[:, 64 * k:64 * k + 64], T.qs[:, at:at + 64]
+            tr.append(RemoteDMATransfer(dst_ids=dst(q), dma_engine_mask=masks[q], remote_sem=S.arr_a if near(q) else S.arr_b, src=a, dst=b))
+        g.remote_dma_fused(tr, local_sem=S.local)
+    g.wait_ge(S.local, 3 * (n_near + n_away))
+
+    V.wait_ge(S.s, j_pb)
+    i = v(V.tensor_copy(T.gs[:, 0:512], T.pb[:, 0:528].indirect(T.off[:, 0:32])))
+    SC.wait_ge(S.v, i_off)
+    SC.wait_ge(S.s, j_pb)
+    j = s(SC.activation(T.gs[:, 512:1024], T.pb[:, 0:528].indirect(T.off[:, 32:64]), F.Copy))
+    V.wait_ge(S.v, i)
+    V.wait_ge(S.s, j)
+    i = v(V.transpose(T.tg[:], T.gs[:]))
+    V.wait_ge(S.v, i)
+    v(V.tensor_tensor(T.sa[0:32, :], T.tg[0:32, 0:1024:32], T.tg[32:64, 0:1024:32], A.add))
+    i = v(V.tensor_tensor(T.sb[0:32, :], T.tg[64:96, 0:1024:32], T.tg[96:128, 0:1024:32], A.add))
+    V.wait_ge(S.v, i)
+    i = v(V.tensor_tensor(T.sc[0:32, :], T.sa[0:32, :], T.sb[0:32, :], A.add))
+    V.wait_ge(S.v, i)
+    for a in range(4):
+        i_slot = v(V.tensor_copy(T.slot[32 * a:32 * a + 32, :], T.sc[0:32, :]))
+
+    g.tensor.wait_ge(S.v, i_q)
+    pe = {}
+    for h in range(2):
+        if h == 0:
+            g.tensor.wait_ge(S.arr_a, 2 * n_near)
+        else:
+            g.tensor.wait_ge(S.arr_b, 2 * n_away)
+        c = slice(192 + 128 * h, 320 + 128 * h)
+        for o in range(2):
+            k = 2 * o + h
+            g.tensor.matmul_mx(T.prod[:, 512 * k:512 * k + 128], T.wq[:, 128 * o:128 * o + 128], T.wsc[:, 128 * o:128 * o + 128],
+                               T.qx[:, c], T.qs[:, c], True, True).then_inc(S.pe, 1)
+            pe[(o, h)] = len(pe) + 1
+    for h in range(2):
+        V.wait_ge(S.pe, pe[(0, h)])
+        i = v(V.tensor_copy(T.res[:, 128 * h:128 * h + 128], T.prod[:, 512 * h:512 * h + 128]))
+        SC.wait_ge(S.pe, pe[(1, h)])
+        j = s(SC.activation(T.res[:, 256 + 128 * h:384 + 128 * h], T.prod[:, 1024 + 512 * h:1152 + 512 * h], F.Copy))
+
+    V.wait_ge(S.v, i)
+    SC.wait_ge(S.s, j)
+    SC.wait_ge(S.v, i_slot)
+    for e in range(2):
+        c = slice(256 * e, 256 * e + 256)
+        d = slice(512 + 256 * e, 768 + 256 * e)
+        i = v(V.tensor_copy(T.yt[:, c], T.res[:, 0:256].indirect(T.slot[:, 16 * e:16 * e + 16])))
+        j = s(SC.activation(T.yt[:, d], T.res[:, 256:512].indirect(T.slot[:, 16 * e:16 * e + 16]), F.Copy))
+        g.sync.wait_ge(S.v, i)
+        g.sync.dma_start(T.y[:, c], T.yt[:, c]).then_inc(S.y, 16)
+        g.sync.wait_ge(S.s, j)
+        g.sync.dma_start(T.y[:, d], T.yt[:, d]).then_inc(S.y, 16)
+    g.sync.wait_ge(S.y, 64)

@@ -1,10 +1,9 @@
 from concourse.bass import DstId, RemoteDMATransfer
-from concourse.mybir import dt, AluOpType, AxisListType, ActivationFunctionType
+from concourse.mybir import dt, AluOpType, ActivationFunctionType
 
 A = AluOpType
 F = ActivationFunctionType
 ROW = "float16"
-HS = 192
 
 SCRATCH = {
     "wl": ("sbuf", [128, 4], "int32"),
@@ -41,11 +40,9 @@ SCRATCH = {
     "b2": ("sbuf", [128, 512], "bfloat16"),
     "row2": ("sbuf", [128, 512], "bfloat16"),
     "pp": ("sbuf", [128, 512], "bfloat16"),
-    "junk": ("sbuf", [128, 1536], "bfloat16"),
-    "mk3": ("sbuf", [128, 512], "bfloat16"),
-    "mk2": ("sbuf", [128, 336], "bfloat16"),
-    "zz": ("sbuf", [128, 4], "float32"),
-    "xx": ("sbuf", [128, 4], "float32"),
+    "junk": ("sbuf", [128, 1024], "bfloat16"),
+    "mk": ("sbuf", [128, 1024], "bfloat16"),
+    "mks": ("sbuf", [128, 1024], "bfloat16"),
     "req": ("sbuf", [128, 4], "float32"),
     "reqs": ("sbuf", [128, 12], "float32"),
     "lown": ("sbuf", [128, 4], "uint16"),
@@ -64,7 +61,7 @@ SCRATCH = {
     "sc": ("sbuf", [128, 32], "float32"),
     "slot": ("sbuf", [128, 32], "uint16"),
     "xs": ("sbuf", [128, 2048], "bfloat16"),
-    "xp": ("sbuf", [128, 2048], "bfloat16"),
+    "xp": ("sbuf", [128, 2064], "bfloat16"),
     "tile": ("sbuf", [128, 1024], "bfloat16"),
     "wt": ("sbuf", [128, 1024], "bfloat16"),
     "wq": ("sbuf", [128, 256], "float8_e4m3fn_x4"),
@@ -102,7 +99,7 @@ def rank_program(g, core, T, topo):
         share[q] = far[k * w:(k + 1) * w]
     for q in mine:
         if q not in share:
-            share[q] = [e for e in topo.engines(core, cores[q]) if e not in far]
+            share[q] = [e for e in topo.engines(core, cores[q]) if e not in far][::2]
     masks = {q: sum(1 << e for e in share[q]) for q in mine}
     n_near = sum(len(share[q]) for q in mine if near(q))
     n_away = sum(len(share[q]) for q in away)
@@ -123,17 +120,28 @@ def rank_program(g, core, T, topo):
         ins.then_inc(S.s, 1)
         return cnt["s"]
 
-    V, SC, X = g.vector, g.scalar, AxisListType.X
+    V, SC = g.vector, g.scalar
 
     g.sync.dma_start(T.wl[:], T.want[:]).then_inc(S.wl, 16)
     g.sync.dma_start(T.xs[:], T.x[:]).then_inc(S.x, 16)
-    g.sync.dma_start(T.wt[:], T.w[:]).then_inc(S.w, 16)
     for a in range(8):
         g.sync.dma_start(T.wl16[16 * a:16 * a + 16, :], T.want[:]).then_inc(S.wl16, 16)
+    g.sync.dma_start(T.wt[:], T.w[:]).then_inc(S.w, 16)
 
     g.iota(T.pi[:], [[1, 1]], 0, 1).then_inc(S.gi, 1)
     g.iota(T.ci[:], [[16, 4]], 0, 0, allow_small_or_imprecise_dtypes=True).then_inc(S.gi, 1)
     g.iota(T.mi[:], [[-32, 4]], 128, 0, allow_small_or_imprecise_dtypes=True).then_inc(S.gi, 1)
+    n_gi = 6
+    g.iota(T.pb[:, 512:528], [[0, 16]], 0, 0, allow_small_or_imprecise_dtypes=True).then_inc(S.gi, 1)
+    at = [64 * (0 if q == me else 1 + mine.index(q)) - 1 for q in range(4)]
+    both = ((T.qcol, [0, 1, 2, 3]), (T.base, at))
+    for t, val in both:
+        g.iota(t[:], [[0, 1]], val[3], 0, allow_small_or_imprecise_dtypes=True).then_inc(S.gi, 1)
+    for q in (2, 1, 0):
+        g.wait_ge(S.gi, n_gi)
+        for t, val in both:
+            g.affine_select(t[:], t[:], [[0, 1]], A.is_ge, float(val[q]), -32 * (q + 1), 1).then_inc(S.gi, 1)
+        n_gi += 2
     i_z = v(V.memset(T.zeros[:], 0.0))
     V.wait_ge(S.gi, 3)
     v(V.tensor_scalar(T.i31[:], T.pi[:], 31, None, A.bitwise_and))
@@ -143,16 +151,16 @@ def rank_program(g, core, T, topo):
     v(V.tensor_copy(T.i31f[:], T.i31[:]))
     i = v(V.tensor_copy(T.i15f[:], T.i15[:]))
     v(V.memset(T.ones[:], 1.0))
+    v(V.memset(T.xp[:, 2048:2064], 0.0))
     V.wait_ge(S.v, i)
     i = v(V.tensor_scalar(T.mp[:], T.mi[:], T.i31f[:, 0:1], None, A.subtract))
     v(V.tensor_scalar(T.s4[:], T.ci[:], T.i15f[:, 0:1], None, A.add))
     v(V.tensor_scalar(T.sb4[:], T.ci[:], T.i15f[:, 0:1], 0.5, A.add, A.add))
     V.wait_ge(S.v, i)
-    i_const = v(V.tensor_scalar(T.kc[:], T.mp[:], -4096.0, 64.0, A.mult, A.add))
-    i_win = v(V.memset(T.win[:, 0:1056], 0.0))
+    v(V.tensor_scalar(T.kc[:], T.mp[:], -4096.0, 64.0, A.mult, A.add))
     SC.wait_ge(S.v, i_z)
-    for k in range(2):
-        j_win = s(SC.activation(T.win[:, 1056 + 528 * k:1584 + 528 * k], T.zeros[:], F.Copy))
+    for k in range(4):
+        j_win = s(SC.activation(T.win[:, 528 * k:528 * k + 528], T.zeros[:], F.Copy))
 
     V.wait_ge(S.wl, 16)
     i = v(V.tensor_copy(T.wf[:], T.wl[:]))
@@ -177,44 +185,39 @@ def rank_program(g, core, T, topo):
     V.wait_ge(S.v, i)
     i = v(V.transpose(T.wint[:], T.win[:, 64:2112]))
     V.wait_ge(S.v, i)
-    i = v(V.tensor_tensor(T.eo[:], T.wint[:, 0:2048:32], T.wint[:, 16:2048:32], A.add))
+    i = v(V.tensor_tensor(T.eo[:], T.wint[:, 0:2048:32], T.wint[:, 16:2048:32], A.max))
     V.wait_ge(S.v, i)
-    v(V.tensor_tensor(T.e01[0:32, :], T.eo[0:32, :], T.eo[32:64, :], A.add))
-    i = v(V.tensor_tensor(T.e23[0:32, :], T.eo[64:96, :], T.eo[96:128, :], A.add))
+    v(V.tensor_tensor(T.e01[0:32, :], T.eo[0:32, :], T.eo[32:64, :], A.max))
+    i = v(V.tensor_tensor(T.e23[0:32, :], T.eo[64:96, :], T.eo[96:128, :], A.max))
     V.wait_ge(S.v, i)
     for q in range(4):
         c = slice(16 * q, 16 * q + 16)
-        i_cn = v(V.tensor_tensor(T.cn[32 * q:32 * q + 32, :], T.e01[0:32, c], T.e23[0:32, c], A.add))
+        i_cn = v(V.tensor_tensor(T.cn[32 * q:32 * q + 32, :], T.e01[0:32, c], T.e23[0:32, c], A.max))
     SC.wait_ge(S.v, i_cn)
     for b in range(8, 16):
-        j = s(SC.activation(T.b2[:, 32 * b:32 * b + 32], T.zeros[:, 0:32], F.Sign, bias=T.cn[:, b:b + 1]))
+        j = s(SC.activation(T.b2[:, 32 * b:32 * b + 32], T.zeros[:, 0:32], F.Identity, bias=T.cn[:, b:b + 1]))
     V.wait_ge(S.v, i_cn)
     for b in range(8):
-        i = v(V.tensor_scalar(T.b2[:, 32 * b:32 * b + 32], T.zeros[:, 0:32], T.cn[:, b:b + 1], 1.0, A.add, A.min))
+        i = v(V.tensor_scalar(T.b2[:, 32 * b:32 * b + 32], T.zeros[:, 0:32], T.cn[:, b:b + 1], None, A.add))
     V.wait_ge(S.v, i)
     V.wait_ge(S.s, j)
     i = v(V.transpose(T.row2[:], T.b2[:]))
-    v(V.memset(T.mk2[:, 512 - HS:513 - HS], float(HS)))
-    v(V.memset(T.xx[:, 0:2], 512.0))
-    v(V.memset(T.zz[:, 3:4], 0.0))
     V.wait_ge(S.v, i)
     i_p = v(V.tensor_tensor_scan(T.pp[:], T.row2[:], T.zeros[:, 0:512], 0.0, A.add, A.add))
 
     SC.wait_ge(S.v, i_p)
-    for c in range(3):
-        n = 512 if c < 2 else HS
-        j_cnt = s(SC.activation(T.junk[:, 512 * c:512 * c + n], T.pp[:, 0:n], F.Sign, bias=T.sb4[:, c:c + 1], scale=-1.0, accum_out=T.zz[:, c:c + 1]))
+    for c in range(2):
+        j_cnt = s(SC.activation(T.junk[:, 512 * c:512 * c + 512], T.pp[:], F.Sign, bias=T.sb4[:, c:c + 1], scale=-1.0, accum_out=T.req[:, c:c + 1]))
     V.wait_ge(S.v, i_p)
-    i3 = v(V.tensor_scalar(T.mk3[:], T.pp[:], T.s4[:, 3:4], 2.0, A.is_le, A.mult))
-    i2 = v(V.tensor_scalar(T.mk2[:, 0:512 - HS], T.pp[:, HS:512], T.s4[:, 2:3], 2.0, A.is_le, A.mult))
-    V.wait_ge(S.v, i3)
-    v(V.tensor_reduce(T.xx[:, 3:4], T.mk3[:], X, A.add))
-    V.wait_ge(S.v, i2)
-    i = v(V.tensor_reduce(T.xx[:, 2:3], T.mk2[:, 0:513 - HS], X, A.add))
+    m = [v(V.tensor_scalar(T.mk[:, 512 * c:512 * c + 512], T.pp[:], T.s4[:, 2 + c:3 + c], 2.0, A.is_le, A.mult)) for c in range(2)]
+    for c in range(4):
+        V.wait_ge(S.v, m[c // 2])
+        k = slice(256 * c, 256 * c + 256)
+        i = v(V.tensor_tensor_scan(T.mks[:, k], T.mk[:, k], T.zeros[:, 0:256], -256.0, A.add, A.add))
     V.wait_ge(S.v, i)
-    V.wait_ge(S.s, j_cnt)
-    i_req = v(V.tensor_tensor(T.req[:], T.zz[:], T.xx[:], A.add))
+    i_req = v(V.tensor_tensor(T.req[:, 2:4], T.mks[:, 255:1024:512], T.mks[:, 511:1024:512], A.add))
 
+    g.wait_ge(S.s, j_cnt)
     g.wait_ge(S.v, i_req)
     tr = []
     for q in mine:
@@ -226,27 +229,24 @@ def rank_program(g, core, T, topo):
     V.wait_ge(S.x, 16)
     SC.wait_ge(S.x, 16)
     for t in range(2):
-        i_xp = v(V.tensor_copy(T.xp[:, 512 * t:512 * t + 512], T.xs[:, t:2048:4]))
+        v(V.tensor_copy(T.xp[:, 512 * t:512 * t + 512], T.xs[:, t:2048:4]))
     for t in range(2, 4):
         j_xp = s(SC.activation(T.xp[:, 512 * t:512 * t + 512], T.xs[:, t:2048:4], F.Copy))
     V.wait_ge(S.v, i_req)
+    V.wait_ge(S.s, j_cnt)
     for a in range(4):
-        i_own = v(V.tensor_scalar(T.lown[32 * a:32 * a + 32, :], T.req[32 * me:32 * me + 32, :], 0.5, 511.0, A.mult, A.min))
+        i_own = v(V.tensor_scalar(T.lown[32 * a:32 * a + 32, :], T.req[32 * me:32 * me + 32, :], 0.5, 256.0, A.mult, A.add))
     V.wait_ge(S.v, i_own)
+    V.wait_ge(S.s, j_xp - 1)
     for t in range(2):
-        v(V.tensor_copy(T.tile[:, 768 + t:1024:4], T.xp[:, 512 * t:512 * t + 512].indirect(T.lown[:, 0:4])))
+        v(V.tensor_copy(T.tile[:, 768 + t:1024:4], T.xp[:, 512 * t:512 * t + 528].indirect(T.lown[:, 0:4])))
     SC.wait_ge(S.s, j_xp)
     SC.wait_ge(S.v, i_own)
     for t in range(2, 4):
-        s(SC.activation(T.tile[:, 768 + t:1024:4], T.xp[:, 512 * t:512 * t + 512].indirect(T.lown[:, 0:4]), F.Copy))
+        s(SC.activation(T.tile[:, 768 + t:1024:4], T.xp[:, 512 * t:512 * t + 528].indirect(T.lown[:, 0:4]), F.Copy))
     V.wait_ge(S.w, 16)
-    i_wq = v(V.quantize_mx(T.wq[:, 0:256], T.wsc[:, 0:256], T.wt[:]))
-    for q in range(4):
-        p = slice(32 * q, 32 * q + 32)
-        v(V.memset(T.qcol[p, :], float(q)))
-        k = 0 if q == me else 1 + mine.index(q)
-        i_base = v(V.memset(T.base[p, :], 64.0 * k - 1.0))
-    v(V.memset(T.pb[:, 512:528], 0.0))
+    v(V.quantize_mx(T.wq[:, 0:256], T.wsc[:, 0:256], T.wt[:]))
+    V.wait_ge(S.gi, n_gi)
     V.wait_ge(S.wl16, 128)
     v(V.tensor_scalar(T.nn[:], T.wl16[:], 511, None, A.bitwise_and))
     i = v(V.tensor_scalar(T.qd[:], T.wl16[:], 9, None, A.logical_shift_right))
@@ -258,18 +258,18 @@ def rank_program(g, core, T, topo):
     V.wait_ge(S.v, i)
     v(V.tensor_scalar(T.off[:, 0:64:2], T.pm[:], 512.0, None, A.add))
     i_off = v(V.tensor_scalar(T.off[:, 1:64:2], T.pm[:], 512.0, None, A.add))
-    SC.wait_ge(S.v, i_base)
+    SC.wait_ge(S.gi, n_gi)
     j_pb = s(SC.activation(T.pb[:, 0:512], T.pp[:], F.Identity, bias=T.base[:, 0:1]))
 
     V.wait_ge(S.lists, n_near + n_away)
     for a in range(4):
-        i_l = v(V.tensor_scalar(T.lrecv[32 * a:32 * a + 32, :], T.reqs[32 * me:32 * me + 32, :], 0.5, 511.0, A.mult, A.min))
+        i_l = v(V.tensor_scalar(T.lrecv[32 * a:32 * a + 32, :], T.reqs[32 * me:32 * me + 32, :], 0.5, 256.0, A.mult, A.add))
     SC.wait_ge(S.v, i_l)
     V.wait_ge(S.v, i_l)
     for t in range(2):
-        i = v(V.tensor_copy(T.tile[:, t:768:4], T.xp[:, 512 * t:512 * t + 512].indirect(T.lrecv[:, 0:12])))
+        i = v(V.tensor_copy(T.tile[:, t:768:4], T.xp[:, 512 * t:512 * t + 528].indirect(T.lrecv[:, 0:12])))
     for t in range(2, 4):
-        j = s(SC.activation(T.tile[:, t:768:4], T.xp[:, 512 * t:512 * t + 512].indirect(T.lrecv[:, 0:12]), F.Copy))
+        j = s(SC.activation(T.tile[:, t:768:4], T.xp[:, 512 * t:512 * t + 528].indirect(T.lrecv[:, 0:12]), F.Copy))
     V.wait_ge(S.v, i)
     V.wait_ge(S.s, j)
     i_q = v(V.quantize_mx(T.qx[:, 0:256], T.qs[:, 0:256], T.tile[:]))
@@ -288,6 +288,7 @@ def rank_program(g, core, T, topo):
     g.wait_ge(S.local, 3 * (n_near + n_away))
 
     V.wait_ge(S.s, j_pb)
+    V.wait_ge(S.v, i_off)
     i = v(V.tensor_copy(T.gs[:, 0:512], T.pb[:, 0:528].indirect(T.off[:, 0:32])))
     SC.wait_ge(S.v, i_off)
     SC.wait_ge(S.s, j_pb)
@@ -302,7 +303,7 @@ def rank_program(g, core, T, topo):
     i = v(V.tensor_tensor(T.sc[0:32, :], T.sa[0:32, :], T.sb[0:32, :], A.add))
     V.wait_ge(S.v, i)
     for a in range(4):
-        i_slot = v(V.tensor_copy(T.slot[32 * a:32 * a + 32, :], T.sc[0:32, :]))
+        v(V.tensor_copy(T.slot[32 * a:32 * a + 32, :], T.sc[0:32, :]))
 
     g.tensor.wait_ge(S.v, i_q)
     pe = {}
@@ -323,16 +324,19 @@ def rank_program(g, core, T, topo):
         SC.wait_ge(S.pe, pe[(1, h)])
         j = s(SC.activation(T.res[:, 256 + 128 * h:384 + 128 * h], T.prod[:, 1024 + 512 * h:1152 + 512 * h], F.Copy))
 
-    V.wait_ge(S.v, i)
-    SC.wait_ge(S.s, j)
-    SC.wait_ge(S.v, i_slot)
-    for e in range(2):
-        c = slice(256 * e, 256 * e + 256)
-        d = slice(512 + 256 * e, 768 + 256 * e)
-        i = v(V.tensor_copy(T.yt[:, c], T.res[:, 0:256].indirect(T.slot[:, 16 * e:16 * e + 16])))
-        j = s(SC.activation(T.yt[:, d], T.res[:, 256:512].indirect(T.slot[:, 16 * e:16 * e + 16]), F.Copy))
-        g.sync.wait_ge(S.v, i)
-        g.sync.dma_start(T.y[:, c], T.yt[:, c]).then_inc(S.y, 16)
-        g.sync.wait_ge(S.s, j)
-        g.sync.dma_start(T.y[:, d], T.yt[:, d]).then_inc(S.y, 16)
+    for e in range(4):
+        o, k = e // 2, 16 * (e % 2)
+        c = 256 * e
+        r = slice(256 * o, 256 * o + 256)
+        if e == 0:
+            V.wait_ge(S.v, i)
+            SC.wait_ge(S.v, i)
+        if e == 2:
+            V.wait_ge(S.s, j)
+            SC.wait_ge(S.s, j)
+        a = v(V.tensor_copy(T.yt[:, c:c + 128], T.res[:, r].indirect(T.slot[:, k:k + 8])))
+        b = s(SC.activation(T.yt[:, c + 128:c + 256], T.res[:, r].indirect(T.slot[:, k + 8:k + 16]), F.Copy))
+        g.sync.wait_ge(S.v, a)
+        g.sync.wait_ge(S.s, b)
+        g.sync.dma_start(T.y[:, c:c + 256], T.yt[:, c:c + 256]).then_inc(S.y, 16)
     g.sync.wait_ge(S.y, 64)

@@ -10,39 +10,41 @@ SCRATCH = {
     "wl16": ("sbuf", [128, 32], "int32"),
     "pi": ("sbuf", [128, 1], "int32"),
     "ci": ("sbuf", [128, 4], "float32"),
-    "mi": ("sbuf", [128, 4], "float32"),
     "i31": ("sbuf", [128, 1], "int32"),
     "i15": ("sbuf", [128, 1], "int32"),
     "i31f": ("sbuf", [128, 1], "float32"),
     "i15f": ("sbuf", [128, 1], "float32"),
-    "mp": ("sbuf", [128, 4], "float32"),
-    "kc": ("sbuf", [128, 4], "float32"),
-    "kk": ("sbuf", [128, 4], "float32"),
-    "s4": ("sbuf", [128, 4], "float32"),
-    "sb4": ("sbuf", [128, 4], "float32"),
+    "lr": ("sbuf", [128, 32], "bfloat16"),
+    "d1": ("sbuf", [128, 320], "bfloat16"),
+    "s4b": ("sbuf", [128, 4], "float32"),
+    "lo": ("sbuf", [128, 2], "float32"),
+    "hi": ("sbuf", [128, 2], "float32"),
+    "ini": ("sbuf", [128, 2], "float32"),
+    "nb": ("sbuf", [128, 2], "float32"),
+    "twos": ("sbuf", [128, 32], "bfloat16"),
     "qcol": ("sbuf", [128, 1], "float32"),
     "base": ("sbuf", [128, 1], "float32"),
-    "zeros": ("sbuf", [128, 528], "bfloat16"),
-    "big": ("sbuf", [128, 512], "bfloat16"),
+    "base1": ("sbuf", [128, 1], "float32"),
+    "zeros": ("sbuf", [128, 512], "bfloat16"),
     "ones": ("sbuf", [128, 64], "bfloat16"),
     "wf": ("sbuf", [128, 4], "float32"),
     "b1": ("sbuf", [128, 128], ROW),
     "row": ("sbuf", [128, 128], ROW),
-    "ne": ("sbuf", [128, 512], "bfloat16"),
-    "dist": ("sbuf", [128, 512], "bfloat16"),
+    "ne": ("sbuf", [128, 320], "bfloat16"),
+    "dist": ("sbuf", [128, 320], "bfloat16"),
     "soff": ("sbuf", [128, 4], "uint16"),
     "win": ("sbuf", [128, 2112], "bfloat16"),
     "wint": ("sbuf", [128, 2048], "bfloat16"),
     "eo": ("sbuf", [128, 64], "float32"),
-    "e01": ("sbuf", [128, 64], "float32"),
-    "e23": ("sbuf", [128, 64], "float32"),
+    "e2": ("sbuf", [128, 64], "float32"),
     "cn": ("sbuf", [128, 16], "float32"),
     "b2": ("sbuf", [128, 512], "bfloat16"),
-    "row2": ("sbuf", [128, 512], "bfloat16"),
-    "pp": ("sbuf", [128, 512], "bfloat16"),
-    "junk": ("sbuf", [128, 1024], "bfloat16"),
-    "mk": ("sbuf", [128, 1024], "bfloat16"),
-    "mks": ("sbuf", [128, 1024], "bfloat16"),
+    "row2": ("sbuf", [128, 544], "bfloat16"),
+    "pp": ("sbuf", [128, 256], "bfloat16"),
+    "po": ("sbuf", [128, 272], "bfloat16"),
+    "junk": ("sbuf", [128, 512], "bfloat16"),
+    "mk": ("sbuf", [128, 512], "bfloat16"),
+    "mks": ("sbuf", [128, 512], "bfloat16"),
     "req": ("sbuf", [128, 4], "float32"),
     "reqs": ("sbuf", [128, 12], "float32"),
     "lown": ("sbuf", [128, 4], "uint16"),
@@ -130,7 +132,7 @@ def rank_program(g, core, T, topo):
 
     g.iota(T.pi[:], [[1, 1]], 0, 1).then_inc(S.gi, 1)
     g.iota(T.ci[:], [[16, 4]], 0, 0, allow_small_or_imprecise_dtypes=True).then_inc(S.gi, 1)
-    g.iota(T.mi[:], [[-32, 4]], 128, 0, allow_small_or_imprecise_dtypes=True).then_inc(S.gi, 1)
+    g.iota(T.lr[:], [[1, 32]], 0, 0, allow_small_or_imprecise_dtypes=True).then_inc(S.gi, 1)
     n_gi = 6
     g.iota(T.pb[:, 512:528], [[0, 16]], 0, 0, allow_small_or_imprecise_dtypes=True).then_inc(S.gi, 1)
     at = [64 * (0 if q == me else 1 + mine.index(q)) - 1 for q in range(4)]
@@ -143,24 +145,31 @@ def rank_program(g, core, T, topo):
             g.affine_select(t[:], t[:], [[0, 1]], A.is_ge, float(val[q]), -32 * (q + 1), 1).then_inc(S.gi, 1)
         n_gi += 2
     i_z = v(V.memset(T.zeros[:], 0.0))
+    v(V.memset(T.d1[:], 4096.0))
     V.wait_ge(S.gi, 3)
     v(V.tensor_scalar(T.i31[:], T.pi[:], 31, None, A.bitwise_and))
     i = v(V.tensor_scalar(T.i15[:], T.pi[:], 15, None, A.bitwise_and))
-    v(V.memset(T.big[:], 4096.0))
+    v(V.memset(T.ones[:], 1.0))
     V.wait_ge(S.v, i)
     v(V.tensor_copy(T.i31f[:], T.i31[:]))
     i = v(V.tensor_copy(T.i15f[:], T.i15[:]))
-    v(V.memset(T.ones[:], 1.0))
-    v(V.memset(T.xp[:, 2048:2064], 0.0))
     V.wait_ge(S.v, i)
-    i = v(V.tensor_scalar(T.mp[:], T.mi[:], T.i31f[:, 0:1], None, A.subtract))
-    v(V.tensor_scalar(T.s4[:], T.ci[:], T.i15f[:, 0:1], None, A.add))
-    v(V.tensor_scalar(T.sb4[:], T.ci[:], T.i15f[:, 0:1], 0.5, A.add, A.add))
-    V.wait_ge(S.v, i)
-    v(V.tensor_scalar(T.kc[:], T.mp[:], -4096.0, 64.0, A.mult, A.add))
+    start = [0, 128, 224, 288]
+    for c in range(3):
+        v(V.tensor_scalar(T.d1[:, start[c]:start[c] + 32], T.lr[:], T.i31f[:, 0:1], -4096.0 * (96 - 32 * c), A.is_equal, A.mult))
+    v(V.tensor_scalar(T.d1[:, 288:319], T.lr[:, 0:31], T.i31f[:, 0:1], -4096.0, A.is_equal, A.mult))
+    v(V.tensor_scalar(T.d1[:, 319:320], T.i31f[:], 31.0, 4096.0, A.not_equal, A.mult))
+    i_s4 = v(V.tensor_scalar(T.s4b[:], T.ci[:], T.i15f[:, 0:1], 2048.0, A.add, A.add))
     SC.wait_ge(S.v, i_z)
     for k in range(4):
-        j_win = s(SC.activation(T.win[:, 528 * k:528 * k + 528], T.zeros[:], F.Copy))
+        j_win = s(SC.activation(T.win[:, 512 * k:512 * k + 512], T.zeros[:], F.Copy))
+    s(SC.activation(T.row2[:, 0:32], T.zeros[:, 0:32], F.Copy))
+    s(SC.activation(T.twos[:], T.zeros[:, 0:32], F.Identity, bias=2.0))
+    SC.wait_ge(S.v, i_s4)
+    s(SC.activation(T.nb[:], T.s4b[:, 0:2], F.Identity, bias=4095.0, scale=-2.0))
+    s(SC.activation(T.lo[:], T.s4b[:, 2:4], F.Identity, bias=-4096.0, scale=2.0))
+    s(SC.activation(T.hi[:], T.s4b[:, 2:4], F.Identity, bias=-4094.0, scale=2.0))
+    j_con = s(SC.activation(T.ini[:], T.s4b[:, 2:4], F.Identity, bias=1048320.0, scale=-512.0))
 
     V.wait_ge(S.wl, 16)
     i = v(V.tensor_copy(T.wf[:], T.wl[:]))
@@ -169,53 +178,55 @@ def rank_program(g, core, T, topo):
         i = v(V.tensor_scalar(T.b1[:, 32 * c:32 * c + 32], T.zeros[:, 0:32], T.wf[:, c:c + 1], None, A.add))
     V.wait_ge(S.v, i)
     i = v(V.transpose(T.row[:], T.b1[:]))
-    v(V.tensor_tensor(T.kk[:], T.wf[:], T.kc[:], A.add))
     V.wait_ge(S.v, i)
     for c in range(4):
-        i = v(V.tensor_scalar(T.ne[:, 128 * c:128 * c + 128], T.row[:], T.wf[:, c:c + 1], None, A.not_equal))
+        i = v(V.tensor_scalar(T.ne[:, start[c]:start[c] + 128 - 32 * c], T.row[:, 32 * c:128], T.wf[:, c:c + 1], None, A.not_equal))
     V.wait_ge(S.v, i)
-    i = v(V.tensor_tensor_scan(T.dist[:], T.ne[:], T.big[:], 0.0, A.mult, A.add))
+    i = v(V.tensor_tensor_scan(T.dist[:], T.ne[:], T.d1[:], 0.0, A.mult, A.add))
     V.wait_ge(S.v, i)
     for c in range(4):
-        i = v(V.tensor_scalar(T.soff[:, c:c + 1], T.dist[:, 128 * c + 127:128 * c + 128], T.kk[:, c:c + 1], T.s4[:, c:c + 1], A.add, A.max))
+        k = start[c] + 127 - 32 * c
+        i = v(V.tensor_scalar(T.soff[:, c:c + 1], T.dist[:, k:k + 1], T.wf[:, c:c + 1], T.s4b[:, c:c + 1], A.add, A.min))
     V.wait_ge(S.v, i)
     V.wait_ge(S.s, j_win)
     i = v(V.tensor_copy(T.win[:, 0:2112].indirect(T.soff[:, 0:4]), T.ones[:]))
 
     V.wait_ge(S.v, i)
-    i = v(V.transpose(T.wint[:], T.win[:, 64:2112]))
+    i = v(V.transpose(T.wint[:], T.win[:, 0:2048]))
     V.wait_ge(S.v, i)
     i = v(V.tensor_tensor(T.eo[:], T.wint[:, 0:2048:32], T.wint[:, 16:2048:32], A.max))
     V.wait_ge(S.v, i)
-    v(V.tensor_tensor(T.e01[0:32, :], T.eo[0:32, :], T.eo[32:64, :], A.max))
-    i = v(V.tensor_tensor(T.e23[0:32, :], T.eo[64:96, :], T.eo[96:128, :], A.max))
+    i = v(V.tensor_tensor(T.e2[0:64, :], T.eo[0:64, :], T.eo[64:128, :], A.max))
     V.wait_ge(S.v, i)
     for q in range(4):
         c = slice(16 * q, 16 * q + 16)
-        i_cn = v(V.tensor_tensor(T.cn[32 * q:32 * q + 32, :], T.e01[0:32, c], T.e23[0:32, c], A.max))
+        i_cn = v(V.tensor_tensor(T.cn[32 * q:32 * q + 32, :], T.e2[0:32, c], T.e2[32:64, c], A.max))
     SC.wait_ge(S.v, i_cn)
-    for b in range(8, 16):
-        j = s(SC.activation(T.b2[:, 32 * b:32 * b + 32], T.zeros[:, 0:32], F.Identity, bias=T.cn[:, b:b + 1]))
+    for b in range(7):
+        j = s(SC.activation(T.b2[:, 32 * b:32 * b + 32], T.zeros[:, 0:32], F.Identity, bias=T.cn[:, 8 + b:9 + b]))
     V.wait_ge(S.v, i_cn)
+    V.wait_ge(S.s, j_con)
+    v(V.tensor_scalar(T.b2[:, 224:256], T.zeros[:, 0:32], T.cn[:, 15:16], None, A.add))
     for b in range(8):
-        i = v(V.tensor_scalar(T.b2[:, 32 * b:32 * b + 32], T.zeros[:, 0:32], T.cn[:, b:b + 1], None, A.add))
+        i = v(V.tensor_scalar(T.b2[:, 256 + 32 * b:288 + 32 * b], T.twos[:], T.cn[:, b:b + 1], T.cn[:, 8 + b:9 + b], A.mult, A.add))
     V.wait_ge(S.v, i)
     V.wait_ge(S.s, j)
-    i = v(V.transpose(T.row2[:], T.b2[:]))
+    i = v(V.transpose(T.row2[:, 32:544], T.b2[:]))
     V.wait_ge(S.v, i)
-    i_p = v(V.tensor_tensor_scan(T.pp[:], T.row2[:], T.zeros[:, 0:512], 0.0, A.add, A.add))
+    i_p = v(V.tensor_tensor_scan(T.pp[:], T.row2[:, 288:544], T.row2[:, 31:287], 0.0, A.add, A.add))
 
+    SC.wait_ge(S.s, j_con)
     SC.wait_ge(S.v, i_p)
     for c in range(2):
-        j_cnt = s(SC.activation(T.junk[:, 512 * c:512 * c + 512], T.pp[:], F.Sign, bias=T.sb4[:, c:c + 1], scale=-1.0, accum_out=T.req[:, c:c + 1]))
+        j_cnt = s(SC.activation(T.junk[:, 256 * c:256 * c + 256], T.pp[:], F.Sign, bias=T.nb[:, c:c + 1], accum_out=T.req[:, c:c + 1]))
     V.wait_ge(S.v, i_p)
-    m = [v(V.tensor_scalar(T.mk[:, 512 * c:512 * c + 512], T.pp[:], T.s4[:, 2 + c:3 + c], 2.0, A.is_le, A.mult)) for c in range(2)]
-    for c in range(4):
-        V.wait_ge(S.v, m[c // 2])
+    m = [v(V.tensor_scalar(T.mk[:, 256 * c:256 * c + 256], T.pp[:], T.lo[:, c:c + 1], T.hi[:, c:c + 1], A.max, A.min)) for c in range(2)]
+    for c in range(2):
+        V.wait_ge(S.v, m[c])
         k = slice(256 * c, 256 * c + 256)
-        i = v(V.tensor_tensor_scan(T.mks[:, k], T.mk[:, k], T.zeros[:, 0:256], -256.0, A.add, A.add))
+        i = v(V.tensor_tensor_scan(T.mks[:, k], T.mk[:, k], T.zeros[:, 0:256], T.ini[:, c:c + 1], A.add, A.add))
     V.wait_ge(S.v, i)
-    i_req = v(V.tensor_tensor(T.req[:, 2:4], T.mks[:, 255:1024:512], T.mks[:, 511:1024:512], A.add))
+    i_req = v(V.tensor_copy(T.req[:, 2:4], T.mks[:, 255:512:256]))
 
     g.wait_ge(S.s, j_cnt)
     g.wait_ge(S.v, i_req)
@@ -229,15 +240,20 @@ def rank_program(g, core, T, topo):
     V.wait_ge(S.x, 16)
     SC.wait_ge(S.x, 16)
     for t in range(2):
-        v(V.tensor_copy(T.xp[:, 512 * t:512 * t + 512], T.xs[:, t:2048:4]))
+        for o in range(2):
+            v(V.tensor_copy(T.xp[:, 512 * t + o:512 * t + 512:2], T.xs[:, 1024 * o + t:1024 * o + 1024:4]))
     for t in range(2, 4):
-        j_xp = s(SC.activation(T.xp[:, 512 * t:512 * t + 512], T.xs[:, t:2048:4], F.Copy))
+        for o in range(2):
+            j_xp = s(SC.activation(T.xp[:, 512 * t + o:512 * t + 512:2], T.xs[:, 1024 * o + t:1024 * o + 1024:4], F.Copy))
+    v(V.memset(T.xp[:, 2048:2064], 0.0))
+    i = v(V.memset(T.po[:, 0:16], 0.0))
+    i_po = v(V.tensor_tensor_scan(T.po[:, 16:272], T.row2[:, 288:544], T.row2[:, 32:288], 0.0, A.add, A.add))
     V.wait_ge(S.v, i_req)
     V.wait_ge(S.s, j_cnt)
     for a in range(4):
-        i_own = v(V.tensor_scalar(T.lown[32 * a:32 * a + 32, :], T.req[32 * me:32 * me + 32, :], 0.5, 256.0, A.mult, A.add))
+        i_own = v(V.tensor_scalar(T.lown[32 * a:32 * a + 32, :], T.req[32 * me:32 * me + 32, :], -1.0, 256.0, A.mult, A.add))
     V.wait_ge(S.v, i_own)
-    V.wait_ge(S.s, j_xp - 1)
+    V.wait_ge(S.s, j_xp - 2)
     for t in range(2):
         v(V.tensor_copy(T.tile[:, 768 + t:1024:4], T.xp[:, 512 * t:512 * t + 528].indirect(T.lown[:, 0:4])))
     SC.wait_ge(S.s, j_xp)
@@ -259,11 +275,15 @@ def rank_program(g, core, T, topo):
     v(V.tensor_scalar(T.off[:, 0:64:2], T.pm[:], 512.0, None, A.add))
     i_off = v(V.tensor_scalar(T.off[:, 1:64:2], T.pm[:], 512.0, None, A.add))
     SC.wait_ge(S.gi, n_gi)
-    j_pb = s(SC.activation(T.pb[:, 0:512], T.pp[:], F.Identity, bias=T.base[:, 0:1]))
+    j = s(SC.activation(T.base1[:], T.base[:], F.Identity, bias=1.0))
+    SC.wait_ge(S.v, i_po)
+    s(SC.activation(T.pb[:, 256:512], T.po[:, 16:272], F.Identity, bias=T.base[:, 0:1], scale=0.5))
+    SC.wait_ge(S.s, j)
+    j_pb = s(SC.activation(T.pb[:, 0:256], T.po[:, 15:271], F.Identity, bias=T.base1[:, 0:1], scale=0.5))
 
     V.wait_ge(S.lists, n_near + n_away)
     for a in range(4):
-        i_l = v(V.tensor_scalar(T.lrecv[32 * a:32 * a + 32, :], T.reqs[32 * me:32 * me + 32, :], 0.5, 256.0, A.mult, A.add))
+        i_l = v(V.tensor_scalar(T.lrecv[32 * a:32 * a + 32, :], T.reqs[32 * me:32 * me + 32, :], -1.0, 256.0, A.mult, A.add))
     SC.wait_ge(S.v, i_l)
     V.wait_ge(S.v, i_l)
     for t in range(2):
@@ -318,11 +338,11 @@ def rank_program(g, core, T, topo):
             g.tensor.matmul_mx(T.prod[:, 512 * k:512 * k + 128], T.wq[:, 128 * o:128 * o + 128], T.wsc[:, 128 * o:128 * o + 128],
                                T.qx[:, c], T.qs[:, c], True, True).then_inc(S.pe, 1)
             pe[(o, h)] = len(pe) + 1
+    SC.wait_ge(S.pe, pe[(1, 0)])
+    s(SC.activation(T.res[:, 256:384], T.prod[:, 1024:1152], F.Copy))
     for h in range(2):
         V.wait_ge(S.pe, pe[(0, h)])
         i = v(V.tensor_copy(T.res[:, 128 * h:128 * h + 128], T.prod[:, 512 * h:512 * h + 128]))
-        SC.wait_ge(S.pe, pe[(1, h)])
-        j = s(SC.activation(T.res[:, 256 + 128 * h:384 + 128 * h], T.prod[:, 1024 + 512 * h:1152 + 512 * h], F.Copy))
 
     for e in range(4):
         o, k = e // 2, 16 * (e % 2)
@@ -336,6 +356,9 @@ def rank_program(g, core, T, topo):
             SC.wait_ge(S.s, j)
         a = v(V.tensor_copy(T.yt[:, c:c + 128], T.res[:, r].indirect(T.slot[:, k:k + 8])))
         b = s(SC.activation(T.yt[:, c + 128:c + 256], T.res[:, r].indirect(T.slot[:, k + 8:k + 16]), F.Copy))
+        if e == 0:
+            SC.wait_ge(S.pe, pe[(1, 1)])
+            j = s(SC.activation(T.res[:, 384:512], T.prod[:, 1536:1664], F.Copy))
         g.sync.wait_ge(S.v, a)
         g.sync.wait_ge(S.s, b)
         g.sync.dma_start(T.y[:, c:c + 256], T.yt[:, c:c + 256]).then_inc(S.y, 16)

from concourse.bass import DstId, RemoteDMATransfer
from concourse.mybir import dt, AluOpType, ActivationFunctionType

A = AluOpType
F = ActivationFunctionType
ROW = "float16"

SCRATCH = {
    "wl": ("sbuf", [128, 4], "int32"),
    "wl16": ("sbuf", [128, 32], "int32"),
    "pi": ("sbuf", [128, 1], "int32"),
    "ci": ("sbuf", [128, 4], "float32"),
    "i31": ("sbuf", [128, 1], "int32"),
    "i15": ("sbuf", [128, 1], "int32"),
    "i31f": ("sbuf", [128, 1], "float32"),
    "i15f": ("sbuf", [128, 1], "float32"),
    "lr": ("sbuf", [128, 32], "bfloat16"),
    "d1": ("sbuf", [128, 320], "bfloat16"),
    "s4b": ("sbuf", [128, 4], "float32"),
    "lo": ("sbuf", [128, 2], "float32"),
    "hi": ("sbuf", [128, 2], "float32"),
    "ini": ("sbuf", [128, 2], "float32"),
    "nb": ("sbuf", [128, 2], "float32"),
    "twos": ("sbuf", [128, 32], "bfloat16"),
    "qcol": ("sbuf", [128, 1], "float32"),
    "base": ("sbuf", [128, 1], "float32"),
    "base1": ("sbuf", [128, 1], "float32"),
    "zeros": ("sbuf", [128, 512], "bfloat16"),
    "ones": ("sbuf", [128, 64], "bfloat16"),
    "wf": ("sbuf", [128, 4], "float32"),
    "b1": ("sbuf", [128, 128], ROW),
    "row": ("sbuf", [128, 128], ROW),
    "ne": ("sbuf", [128, 320], "bfloat16"),
    "dist": ("sbuf", [128, 320], "bfloat16"),
    "soff": ("sbuf", [128, 4], "uint16"),
    "win": ("sbuf", [128, 2112], "bfloat16"),
    "wint": ("sbuf", [128, 2048], "bfloat16"),
    "eo": ("sbuf", [128, 64], "float32"),
    "e2": ("sbuf", [128, 64], "float32"),
    "cn": ("sbuf", [128, 16], "float32"),
    "b2": ("sbuf", [128, 512], "bfloat16"),
    "row2": ("sbuf", [128, 544], "bfloat16"),
    "pp": ("sbuf", [128, 256], "bfloat16"),
    "po": ("sbuf", [128, 272], "bfloat16"),
    "junk": ("sbuf", [128, 512], "bfloat16"),
    "mk": ("sbuf", [128, 512], "bfloat16"),
    "mks": ("sbuf", [128, 512], "bfloat16"),
    "req": ("sbuf", [128, 4], "float32"),
    "reqs": ("sbuf", [128, 12], "float32"),
    "lown": ("sbuf", [128, 4], "uint16"),
    "lrecv": ("sbuf", [128, 12], "uint16"),
    "nn": ("sbuf", [128, 32], "int32"),
    "qd": ("sbuf", [128, 32], "int32"),
    "n5": ("sbuf", [128, 32], "float32"),
    "ee": ("sbuf", [128, 32], "float32"),
    "pm": ("sbuf", [128, 32], "float32"),
    "off": ("sbuf", [128, 64], "uint16"),
    "pb": ("sbuf", [128, 528], "bfloat16"),
    "gs": ("sbuf", [128, 1024], "bfloat16"),
    "tg": ("sbuf", [128, 1024], "bfloat16"),
    "sa": ("sbuf", [128, 32], "float32"),
    "sb": ("sbuf", [128, 32], "float32"),
    "sc": ("sbuf", [128, 32], "float32"),
    "slot": ("sbuf", [128, 32], "uint16"),
    "xs": ("sbuf", [128, 2048], "bfloat16"),
    "xp": ("sbuf", [128, 2064], "bfloat16"),
    "tile": ("sbuf", [128, 1024], "bfloat16"),
    "wt": ("sbuf", [128, 1024], "bfloat16"),
    "wq": ("sbuf", [128, 256], "float8_e4m3fn_x4"),
    "wsc": ("sbuf", [128, 256], "uint8"),
    "qx": ("sbuf", [128, 448], "float8_e4m3fn_x4"),
    "qs": ("sbuf", [128, 448], "uint8"),
    "prod": ("psum", [128, 2048], "float32"),
    "res": ("sbuf", [128, 512], "float32"),
    "yt": ("sbuf", [128, 1024], "float32"),
}
SEMAPHORES = ["v", "s", "pe", "gi", "wl", "wl16", "x", "w", "y", "lists", "local", "arr_a", "arr_b"]


def rank_program(g, core, T, topo):
    me = T.rank_of(core)
    if me is None:
        return
    cores = T.cores
    S = T.sem

    def near(q):
        return topo.chip(cores[q]) == topo.chip(core)

    def order(r):
        o = [q for q in range(len(cores)) if q != r]
        return sorted(o, key=lambda q: (topo.chip(cores[q]) != topo.chip(cores[r]), (q - r) % len(cores)))

    mine = order(me)
    away = [q for q in mine if not near(q)]
    share = {}
    far = []
    for k, q in enumerate(away):
        far = topo.engines(core, cores[q])
        w = len(far) // len(away)
        share[q] = far[k * w:(k + 1) * w]
    for q in mine:
        if q not in share:
            share[q] = [e for e in topo.engines(core, cores[q]) if e not in far][::2]
    masks = {q: sum(1 << e for e in share[q]) for q in mine}
    n_near = sum(len(share[q]) for q in mine if near(q))
    n_away = sum(len(share[q]) for q in away)

    def dst(q):
        rid, pid, _ = topo.addr(cores[q])
        return [DstId(rid=rid, pnc=pid)]

    cnt = {"v": 0, "s": 0}

    def v(ins):
        cnt["v"] += 1
        ins.then_inc(S.v, 1)
        return cnt["v"]

    def s(ins):
        cnt["s"] += 1
        ins.then_inc(S.s, 1)
        return cnt["s"]

    V, SC = g.vector, g.scalar

    g.sync.dma_start(T.wl[:], T.want[:]).then_inc(S.wl, 16)
    g.sync.dma_start(T.xs[:], T.x[:]).then_inc(S.x, 16)
    for a in range(8):
        g.sync.dma_start(T.wl16[16 * a:16 * a + 16, :], T.want[:]).then_inc(S.wl16, 16)
    g.sync.dma_start(T.wt[:], T.w[:]).then_inc(S.w, 16)

    g.iota(T.pi[:], [[1, 1]], 0, 1).then_inc(S.gi, 1)
    g.iota(T.ci[:], [[16, 4]], 0, 0, allow_small_or_imprecise_dtypes=True).then_inc(S.gi, 1)
    g.iota(T.lr[:], [[1, 32]], 0, 0, allow_small_or_imprecise_dtypes=True).then_inc(S.gi, 1)
    n_gi = 6
    g.iota(T.pb[:, 512:528], [[0, 16]], 0, 0, allow_small_or_imprecise_dtypes=True).then_inc(S.gi, 1)
    at = [64 * (0 if q == me else 1 + mine.index(q)) - 1 for q in range(4)]
    both = ((T.qcol, [0, 1, 2, 3]), (T.base, at))
    for t, val in both:
        g.iota(t[:], [[0, 1]], val[3], 0, allow_small_or_imprecise_dtypes=True).then_inc(S.gi, 1)
    for q in (2, 1, 0):
        g.wait_ge(S.gi, n_gi)
        for t, val in both:
            g.affine_select(t[:], t[:], [[0, 1]], A.is_ge, float(val[q]), -32 * (q + 1), 1).then_inc(S.gi, 1)
        n_gi += 2
    i_z = v(V.memset(T.zeros[:], 0.0))
    v(V.memset(T.d1[:], 4096.0))
    V.wait_ge(S.gi, 3)
    v(V.tensor_scalar(T.i31[:], T.pi[:], 31, None, A.bitwise_and))
    i = v(V.tensor_scalar(T.i15[:], T.pi[:], 15, None, A.bitwise_and))
    v(V.memset(T.ones[:], 1.0))
    V.wait_ge(S.v, i)
    v(V.tensor_copy(T.i31f[:], T.i31[:]))
    i = v(V.tensor_copy(T.i15f[:], T.i15[:]))
    V.wait_ge(S.v, i)
    start = [0, 128, 224, 288]
    for c in range(3):
        v(V.tensor_scalar(T.d1[:, start[c]:start[c] + 32], T.lr[:], T.i31f[:, 0:1], -4096.0 * (96 - 32 * c), A.is_equal, A.mult))
    v(V.tensor_scalar(T.d1[:, 288:319], T.lr[:, 0:31], T.i31f[:, 0:1], -4096.0, A.is_equal, A.mult))
    v(V.tensor_scalar(T.d1[:, 319:320], T.i31f[:], 31.0, 4096.0, A.not_equal, A.mult))
    i_s4 = v(V.tensor_scalar(T.s4b[:], T.ci[:], T.i15f[:, 0:1], 2048.0, A.add, A.add))
    SC.wait_ge(S.v, i_z)
    for k in range(4):
        j_win = s(SC.activation(T.win[:, 512 * k:512 * k + 512], T.zeros[:], F.Copy))
    s(SC.activation(T.row2[:, 0:32], T.zeros[:, 0:32], F.Copy))
    s(SC.activation(T.twos[:], T.zeros[:, 0:32], F.Identity, bias=2.0))
    SC.wait_ge(S.v, i_s4)
    s(SC.activation(T.nb[:], T.s4b[:, 0:2], F.Identity, bias=4095.0, scale=-2.0))
    s(SC.activation(T.lo[:], T.s4b[:, 2:4], F.Identity, bias=-4096.0, scale=2.0))
    s(SC.activation(T.hi[:], T.s4b[:, 2:4], F.Identity, bias=-4094.0, scale=2.0))
    j_con = s(SC.activation(T.ini[:], T.s4b[:, 2:4], F.Identity, bias=1048320.0, scale=-512.0))

    V.wait_ge(S.wl, 16)
    i = v(V.tensor_copy(T.wf[:], T.wl[:]))
    V.wait_ge(S.v, i)
    for c in range(4):
        i = v(V.tensor_scalar(T.b1[:, 32 * c:32 * c + 32], T.zeros[:, 0:32], T.wf[:, c:c + 1], None, A.add))
    V.wait_ge(S.v, i)
    i = v(V.transpose(T.row[:], T.b1[:]))
    V.wait_ge(S.v, i)
    for c in range(4):
        i = v(V.tensor_scalar(T.ne[:, start[c]:start[c] + 128 - 32 * c], T.row[:, 32 * c:128], T.wf[:, c:c + 1], None, A.not_equal))
    V.wait_ge(S.v, i)
    i = v(V.tensor_tensor_scan(T.dist[:], T.ne[:], T.d1[:], 0.0, A.mult, A.add))
    V.wait_ge(S.v, i)
    for c in range(4):
        k = start[c] + 127 - 32 * c
        i = v(V.tensor_scalar(T.soff[:, c:c + 1], T.dist[:, k:k + 1], T.wf[:, c:c + 1], T.s4b[:, c:c + 1], A.add, A.min))
    V.wait_ge(S.v, i)
    V.wait_ge(S.s, j_win)
    i = v(V.tensor_copy(T.win[:, 0:2112].indirect(T.soff[:, 0:4]), T.ones[:]))

    V.wait_ge(S.v, i)
    i = v(V.transpose(T.wint[:], T.win[:, 0:2048]))
    V.wait_ge(S.v, i)
    i = v(V.tensor_tensor(T.eo[:], T.wint[:, 0:2048:32], T.wint[:, 16:2048:32], A.max))
    V.wait_ge(S.v, i)
    i = v(V.tensor_tensor(T.e2[0:64, :], T.eo[0:64, :], T.eo[64:128, :], A.max))
    V.wait_ge(S.v, i)
    for q in range(4):
        c = slice(16 * q, 16 * q + 16)
        i_cn = v(V.tensor_tensor(T.cn[32 * q:32 * q + 32, :], T.e2[0:32, c], T.e2[32:64, c], A.max))
    SC.wait_ge(S.v, i_cn)
    for b in range(7):
        j = s(SC.activation(T.b2[:, 32 * b:32 * b + 32], T.zeros[:, 0:32], F.Identity, bias=T.cn[:, 8 + b:9 + b]))
    V.wait_ge(S.v, i_cn)
    V.wait_ge(S.s, j_con)
    v(V.tensor_scalar(T.b2[:, 224:256], T.zeros[:, 0:32], T.cn[:, 15:16], None, A.add))
    for b in range(8):
        i = v(V.tensor_scalar(T.b2[:, 256 + 32 * b:288 + 32 * b], T.twos[:], T.cn[:, b:b + 1], T.cn[:, 8 + b:9 + b], A.mult, A.add))
    V.wait_ge(S.v, i)
    V.wait_ge(S.s, j)
    i = v(V.transpose(T.row2[:, 32:544], T.b2[:]))
    V.wait_ge(S.v, i)
    i_p = v(V.tensor_tensor_scan(T.pp[:], T.row2[:, 288:544], T.row2[:, 31:287], 0.0, A.add, A.add))

    SC.wait_ge(S.s, j_con)
    SC.wait_ge(S.v, i_p)
    for c in range(2):
        j_cnt = s(SC.activation(T.junk[:, 256 * c:256 * c + 256], T.pp[:], F.Sign, bias=T.nb[:, c:c + 1], accum_out=T.req[:, c:c + 1]))
    V.wait_ge(S.v, i_p)
    m = [v(V.tensor_scalar(T.mk[:, 256 * c:256 * c + 256], T.pp[:], T.lo[:, c:c + 1], T.hi[:, c:c + 1], A.max, A.min)) for c in range(2)]
    for c in range(2):
        V.wait_ge(S.v, m[c])
        k = slice(256 * c, 256 * c + 256)
        i = v(V.tensor_tensor_scan(T.mks[:, k], T.mk[:, k], T.zeros[:, 0:256], T.ini[:, c:c + 1], A.add, A.add))
    V.wait_ge(S.v, i)
    i_req = v(V.tensor_copy(T.req[:, 2:4], T.mks[:, 255:512:256]))

    g.wait_ge(S.s, j_cnt)
    g.wait_ge(S.v, i_req)
    tr = []
    for q in mine:
        at = 4 * order(q).index(me)
        tr.append(RemoteDMATransfer(dst_ids=dst(q), dma_engine_mask=masks[q], remote_sem=S.lists,
                                    src=T.req[:], dst=T.reqs[:, at:at + 4]))
    g.remote_dma_fused(tr, local_sem=S.local)

    V.wait_ge(S.x, 16)
    SC.wait_ge(S.x, 16)
    for t in range(2):
        for o in range(2):
            v(V.tensor_copy(T.xp[:, 512 * t + o:512 * t + 512:2], T.xs[:, 1024 * o + t:1024 * o + 1024:4]))
    for t in range(2, 4):
        for o in range(2):
            j_xp = s(SC.activation(T.xp[:, 512 * t + o:512 * t + 512:2], T.xs[:, 1024 * o + t:1024 * o + 1024:4], F.Copy))
    v(V.memset(T.xp[:, 2048:2064], 0.0))
    i = v(V.memset(T.po[:, 0:16], 0.0))
    i_po = v(V.tensor_tensor_scan(T.po[:, 16:272], T.row2[:, 288:544], T.row2[:, 32:288], 0.0, A.add, A.add))
    V.wait_ge(S.v, i_req)
    V.wait_ge(S.s, j_cnt)
    for a in range(4):
        i_own = v(V.tensor_scalar(T.lown[32 * a:32 * a + 32, :], T.req[32 * me:32 * me + 32, :], -1.0, 256.0, A.mult, A.add))
    V.wait_ge(S.v, i_own)
    V.wait_ge(S.s, j_xp - 2)
    for t in range(2):
        v(V.tensor_copy(T.tile[:, 768 + t:1024:4], T.xp[:, 512 * t:512 * t + 528].indirect(T.lown[:, 0:4])))
    SC.wait_ge(S.s, j_xp)
    SC.wait_ge(S.v, i_own)
    for t in range(2, 4):
        s(SC.activation(T.tile[:, 768 + t:1024:4], T.xp[:, 512 * t:512 * t + 528].indirect(T.lown[:, 0:4]), F.Copy))
    V.wait_ge(S.w, 16)
    v(V.quantize_mx(T.wq[:, 0:256], T.wsc[:, 0:256], T.wt[:]))
    V.wait_ge(S.gi, n_gi)
    V.wait_ge(S.wl16, 128)
    v(V.tensor_scalar(T.nn[:], T.wl16[:], 511, None, A.bitwise_and))
    i = v(V.tensor_scalar(T.qd[:], T.wl16[:], 9, None, A.logical_shift_right))
    V.wait_ge(S.v, i)
    v(V.tensor_scalar(T.n5[:], T.nn[:], -512.0, None, A.add))
    i = v(V.tensor_scalar(T.ee[:], T.qd[:], T.qcol[:, 0:1], None, A.is_equal))
    V.wait_ge(S.v, i)
    i = v(V.tensor_tensor(T.pm[:], T.n5[:], T.ee[:], A.mult))
    V.wait_ge(S.v, i)
    v(V.tensor_scalar(T.off[:, 0:64:2], T.pm[:], 512.0, None, A.add))
    i_off = v(V.tensor_scalar(T.off[:, 1:64:2], T.pm[:], 512.0, None, A.add))
    SC.wait_ge(S.gi, n_gi)
    j = s(SC.activation(T.base1[:], T.base[:], F.Identity, bias=1.0))
    SC.wait_ge(S.v, i_po)
    s(SC.activation(T.pb[:, 256:512], T.po[:, 16:272], F.Identity, bias=T.base[:, 0:1], scale=0.5))
    SC.wait_ge(S.s, j)
    j_pb = s(SC.activation(T.pb[:, 0:256], T.po[:, 15:271], F.Identity, bias=T.base1[:, 0:1], scale=0.5))

    V.wait_ge(S.lists, n_near + n_away)
    for a in range(4):
        i_l = v(V.tensor_scalar(T.lrecv[32 * a:32 * a + 32, :], T.reqs[32 * me:32 * me + 32, :], -1.0, 256.0, A.mult, A.add))
    SC.wait_ge(S.v, i_l)
    V.wait_ge(S.v, i_l)
    for t in range(2):
        i = v(V.tensor_copy(T.tile[:, t:768:4], T.xp[:, 512 * t:512 * t + 528].indirect(T.lrecv[:, 0:12])))
    for t in range(2, 4):
        j = s(SC.activation(T.tile[:, t:768:4], T.xp[:, 512 * t:512 * t + 528].indirect(T.lrecv[:, 0:12]), F.Copy))
    V.wait_ge(S.v, i)
    V.wait_ge(S.s, j)
    i_q = v(V.quantize_mx(T.qx[:, 0:256], T.qs[:, 0:256], T.tile[:]))

    g.wait_ge(S.v, i_q)
    for codes in (True, False):
        tr = []
        for k, q in enumerate(mine):
            at = 256 + 64 * order(q).index(me)
            if codes:
                a, b = T.qx[:, 64 * k:64 * k + 64].bitcast(dt.uint8), T.qx[:, at:at + 64].bitcast(dt.uint8)
            else:
                a, b = T.qs[:, 64 * k:64 * k + 64], T.qs[:, at:at + 64]
            tr.append(RemoteDMATransfer(dst_ids=dst(q), dma_engine_mask=masks[q], remote_sem=S.arr_a if near(q) else S.arr_b, src=a, dst=b))
        g.remote_dma_fused(tr, local_sem=S.local)
    g.wait_ge(S.local, 3 * (n_near + n_away))

    V.wait_ge(S.s, j_pb)
    V.wait_ge(S.v, i_off)
    i = v(V.tensor_copy(T.gs[:, 0:512], T.pb[:, 0:528].indirect(T.off[:, 0:32])))
    SC.wait_ge(S.v, i_off)
    SC.wait_ge(S.s, j_pb)
    j = s(SC.activation(T.gs[:, 512:1024], T.pb[:, 0:528].indirect(T.off[:, 32:64]), F.Copy))
    V.wait_ge(S.v, i)
    V.wait_ge(S.s, j)
    i = v(V.transpose(T.tg[:], T.gs[:]))
    V.wait_ge(S.v, i)
    v(V.tensor_tensor(T.sa[0:32, :], T.tg[0:32, 0:1024:32], T.tg[32:64, 0:1024:32], A.add))
    i = v(V.tensor_tensor(T.sb[0:32, :], T.tg[64:96, 0:1024:32], T.tg[96:128, 0:1024:32], A.add))
    V.wait_ge(S.v, i)
    i = v(V.tensor_tensor(T.sc[0:32, :], T.sa[0:32, :], T.sb[0:32, :], A.add))
    V.wait_ge(S.v, i)
    for a in range(4):
        v(V.tensor_copy(T.slot[32 * a:32 * a + 32, :], T.sc[0:32, :]))

    g.tensor.wait_ge(S.v, i_q)
    pe = {}
    for h in range(2):
        if h == 0:
            g.tensor.wait_ge(S.arr_a, 2 * n_near)
        else:
            g.tensor.wait_ge(S.arr_b, 2 * n_away)
        c = slice(192 + 128 * h, 320 + 128 * h)
        for o in range(2):
            k = 2 * o + h
            g.tensor.matmul_mx(T.prod[:, 512 * k:512 * k + 128], T.wq[:, 128 * o:128 * o + 128], T.wsc[:, 128 * o:128 * o + 128],
                               T.qx[:, c], T.qs[:, c], True, True).then_inc(S.pe, 1)
            pe[(o, h)] = len(pe) + 1
    SC.wait_ge(S.pe, pe[(1, 0)])
    s(SC.activation(T.res[:, 256:384], T.prod[:, 1024:1152], F.Copy))
    for h in range(2):
        V.wait_ge(S.pe, pe[(0, h)])
        i = v(V.tensor_copy(T.res[:, 128 * h:128 * h + 128], T.prod[:, 512 * h:512 * h + 128]))

    for e in range(4):
        o, k = e // 2, 16 * (e % 2)
        c = 256 * e
        r = slice(256 * o, 256 * o + 256)
        if e == 0:
            V.wait_ge(S.v, i)
            SC.wait_ge(S.v, i)
        if e == 2:
            V.wait_ge(S.s, j)
            SC.wait_ge(S.s, j)
        a = v(V.tensor_copy(T.yt[:, c:c + 128], T.res[:, r].indirect(T.slot[:, k:k + 8])))
        b = s(SC.activation(T.yt[:, c + 128:c + 256], T.res[:, r].indirect(T.slot[:, k + 8:k + 16]), F.Copy))
        if e == 0:
            SC.wait_ge(S.pe, pe[(1, 1)])
            j = s(SC.activation(T.res[:, 384:512], T.prod[:, 1536:1664], F.Copy))
        g.sync.wait_ge(S.v, a)
        g.sync.wait_ge(S.s, b)
        g.sync.dma_start(T.y[:, c:c + 256], T.yt[:, c:c + 256]).then_inc(S.y, 16)
    g.sync.wait_ge(S.y, 64)
